import numpy as np
import ml_dtypes


def mxq(x, axis, fmt="e4m3"):
    dtype, down = {"e4m3": (ml_dtypes.float8_e4m3fn, 7), "e5m2": (ml_dtypes.float8_e5m2, 14)}[fmt]
    v = np.moveaxis(np.asarray(x, np.float32).astype(ml_dtypes.bfloat16).astype(np.float64), axis, -1)
    blocks = v.reshape(v.shape[:-1] + (-1, 32))
    amax = np.abs(blocks).max(-1, keepdims=True)
    byte = np.maximum(np.where(amax > 0, np.frexp(amax)[1] - 1 + 127, 0) - down, 1)
    scale = np.exp2(byte - 127.0)
    codes = (blocks / scale).astype(np.float32).astype(dtype).astype(np.float64)
    return np.moveaxis((codes * scale).reshape(v.shape), -1, axis)


WIDE = False


def mx_kscale(k):
    if not WIDE:
        return np.ones(k)
    levels = np.array([10, -10, 5, -5, 0])
    if k % 512:
        return np.exp2(np.random.permutation(np.resize(levels, k // 32))).repeat(32)
    a = np.empty((k // 512, 16))
    for p in range(k // 512):
        a[p, :8] = np.random.permutation(np.resize(levels, 8))
        for g in range(8):
            far = levels[np.abs(levels - a[p, g]) >= 10]
            a[p, g + 8] = far[np.random.randint(len(far))]
    return np.exp2(a.ravel()).repeat(32)


def f64(x):
    return np.asarray(x).astype(np.float64)


def striped(idx):
    return np.tile(idx.reshape(-1, 16).T, (8, 1)).astype(np.uint16)


def unstriped(offs):
    return offs[:16].T.reshape(-1).astype(np.int64)


def striped8(idx):
    return np.concatenate([x.reshape(-1, 16).T for x in idx]).astype(np.uint16)


def runs(offs, k):
    lists = np.stack([offs[16 * r : 16 * r + 16].T.reshape(-1) for r in range(8)]).astype(np.int64)
    return lists[np.arange(k) % 512 // 64]


def pack_weight(w):
    k, n = w.shape
    w = f64(np.asarray(w, np.float32).astype(ml_dtypes.bfloat16)).reshape(k // 32, 32, n)
    amax = np.abs(w).max(1)
    byte = np.clip(np.where(amax > 0, np.frexp(amax)[1] - 1 + 127 - 7, 1), 1, 254)
    scaled = (w * np.exp2(127.0 - byte)[:, None, :]).reshape(k, n).astype(np.float32)
    words = np.ascontiguousarray(scaled.reshape(k // 512, 128, 4, n).transpose(0, 1, 3, 2)).astype(ml_dtypes.float8_e4m3fn).view(np.uint8)
    return words, np.ascontiguousarray(byte.astype(np.uint8).reshape(k // 512, 16, n))


def unpack_weight(words, scales):
    g, p, n, _ = words.shape
    vals = np.ascontiguousarray(words).view(ml_dtypes.float8_e4m3fn).astype(np.float64) * np.repeat(np.exp2(scales.astype(np.float64) - 127.0), 8, axis=1)[..., None]
    return vals.transpose(0, 1, 3, 2).reshape(g * 512, n)


def sigmoid(v):
    return 1.0 / (1.0 + np.exp(-np.maximum(v, -700.0)))


K, T, S, N, H, W = 512, 2048, 512, 512, 512, 256


def setup_inputs():
    n = np.random.standard_normal
    s = mx_kscale(K)[:, None]
    u = mx_kscale(S)
    packed_xT = pack_weight(n((K, T)) * s)
    perm = np.stack([np.random.permutation(H) for _ in range(8)])
    return {
        "x_words": packed_xT[0],
        "x_scales": packed_xT[1],
        "wa": (n((K, H)) / np.sqrt(K) / s).astype(np.float32),
        "wb": (n((K, N)) / np.sqrt(K) / s).astype(np.float32),
        "gt": (np.random.uniform(0.5, 1.5, (S, 1)) * u[:, None]).astype(np.float32),
        "gi": (np.random.uniform(0.5, 1.5, (S, 1)) / u[:, None]).astype(np.float32),
        "offs": striped(np.random.permutation(T)[:S]),
        "two": striped(np.random.permutation(T)[:S]),
        "n1": striped8(perm[:, :W]),
        "n2": striped8(perm[:, W:]),
        "n3": striped8(np.stack([np.random.permutation(N) for _ in range(8)])),
        "n4": striped8(np.stack([np.random.permutation(N) for _ in range(8)])),
    }


def reference(x_words, x_scales, wa, wb, gt, gi, offs, two, n1, n2, n3, n4):
    xq = unpack_weight(x_words, x_scales)[:, unstriped(offs)]
    a = xq.T @ mxq(f64(wa), 0, "e4m3")
    pa = a[np.arange(S)[:, None], runs(n1, S)]
    pb = a[np.arange(S)[:, None], runs(n2, S)]
    rb = pa * pb
    ra = pa + pb
    ds = np.zeros((S, H))
    ds[np.arange(S)[:, None], runs(n1, S)] = ra
    dt = ds.copy()
    dt[np.arange(S)[:, None], runs(n2, S)] = rb
    z = f64(gt) * dt
    x_two = unpack_weight(x_words, x_scales)[:, unstriped(two)]
    b = x_two.T @ mxq(f64(wb), 0, "e4m3")
    z2 = f64(gi) * b
    cv = 0.0625 * ((mxq(z, 0, "e4m3").T @ mxq(z2, 0, "e4m3")))
    return (cv - (cv[np.arange(H)[:, None], runs(n3, H)])) * (sigmoid(cv[np.arange(H)[:, None], runs(n4, H)]))

@@ -1,0 +1,282 @@
+from contextlib import ExitStack
+
+import concourse.mybir as mybir
+
+K, T, S, N, H, W = 512, 2048, 512, 512, 512, 256
+FLOPS = 2 * K * S * H + 2 * K * S * N + 2 * S * H * N
+
+F32 = mybir.dt.float32
+BF16 = mybir.dt.bfloat16
+I32 = mybir.dt.int32
+U32 = mybir.dt.uint32
+U16 = mybir.dt.uint16
+U8 = mybir.dt.uint8
+FP8X4 = mybir.dt.float8_e4m3fn_x4
+ACT = mybir.ActivationFunctionType
+ALU = mybir.AluOpType
+
+P = 128
+PACK = 4
+HALF = 256
+VECTOR_COLUMNS = 160
+
+
+def tile_picked_mombondgdif_none_p_kernel(
+    tc, x_words, x_scales, wa, wb, gt, gi, offs, two, n1, n2, n3, n4, out
+):
+    nc = tc.nc
+    with ExitStack() as ctx:
+        keep = ctx.enter_context(tc.tile_pool(name="keep", bufs=1))
+        psum = ctx.enter_context(tc.psum_pool(name="psum", bufs=8))
+
+        def load_list(src, name):
+            tile = keep.tile(list(src.shape), U16, name=name)
+            nc.sync.dma_start(tile[:], src)
+            return tile
+
+        def load_weight_half(w, half, name):
+            tile = keep.tile([P, PACK, HALF], F32, name=name)
+            rows = w.rearrange("(p j) c -> p j c", j=PACK)
+            nc.sync.dma_start(out=tile[:], in_=rows[:, :, half * HALF : (half + 1) * HALF])
+            return tile
+
+        def load_gate(g, name):
+            tile = keep.tile([P, PACK], F32, name=name)
+            nc.sync.dma_start(out=tile[:], in_=g.rearrange("(p t) o -> p (t o)", t=PACK))
+            return tile
+
+        def interleave(copy, dst, src):
+            copy(
+                out=dst.rearrange("p (c i t) -> p c t i", i=4, t=PACK),
+                in_=src.rearrange("p t (c i) -> p c t i", i=4),
+            )
+
+        def quantize(codes, scales, grouped):
+            nc.vector.quantize_mx(out=codes.bitcast(FP8X4), scales=scales, in_=grouped)
+
+        def product(acc, left_codes, left_scales, right_codes, right_scales):
+            nc.tensor.matmul_mx(
+                out=acc,
+                lhsT=left_codes.bitcast(FP8X4),
+                lhsT_scale=left_scales,
+                rhs=right_codes.bitcast(FP8X4),
+                rhs_scale=right_scales,
+                start=True,
+                stop=True,
+            )
+
+        scale_table = keep.tile([P, T], U8, name="scale_table")
+        nc.vector.memset(scale_table[:].bitcast(I32), 0)
+        offs_t = load_list(offs, "offs_t")
+        for q in range(4):
+            nc.sync.dma_start(
+                out=scale_table[32 * q : 32 * q + 4, :].bitcast(I32),
+                in_=x_scales[0, 4 * q : 4 * q + 4, :].bitcast(I32),
+            )
+        wa_raw = [load_weight_half(wa, h, "wa_raw%d" % h) for h in range(2)]
+        word_table = keep.tile([P, T], U32, name="word_table")
+        nc.sync.dma_start(
+            out=word_table[:].bitcast(I32),
+            in_=x_words[0].rearrange("p n t -> p (n t)").bitcast(I32),
+        )
+        two_t = load_list(two, "two_t")
+        n1_t = load_list(n1, "n1_t")
+        n2_t = load_list(n2, "n2_t")
+        wb_raw = keep.tile([P, PACK, N], F32, name="wb_raw", tag="handed_on", align_bytes=64)
+        nc.sync.dma_start(out=wb_raw[:], in_=wb.rearrange("(p j) c -> p j c", j=PACK))
+        gt_t = load_gate(gt, "gt_t")
+        gi_t = load_gate(gi, "gi_t")
+        n4_t = load_list(n4, "n4_t")
+        n3_t = load_list(n3, "n3_t")
+
+        def pick_scales(offsets, name):
+            picked = keep.tile([P, S], U8, name=name + "_picked")
+            nc.vector.tensor_copy(picked[:], scale_table[:].indirect(offsets[:]))
+            return picked
+
+        def deal_scales(picked, name):
+            dealt = keep.tile([P, S], U8, name=name + "_dealt", align_bytes=64)
+            nc.vector.tensor_copy(
+                out=dealt[:].rearrange("p (t m) -> p t m", t=PACK),
+                in_=picked[:].rearrange("p (m t) -> p t m", t=PACK),
+            )
+            return dealt
+
+        def pick_words(offsets, name, tag):
+            dealt = keep.tile([P, S], U32, name=name, tag=tag, align_bytes=64)
+            nc.vector.tensor_copy(
+                dealt[:].rearrange("p (t m) -> p m t", t=PACK), word_table[:].indirect(offsets[:])
+            )
+            return dealt
+
+        xa_picked = pick_scales(offs_t, "xa_scales")
+        xa_scales = deal_scales(xa_picked, "xa_scales")
+
+        wa_grouped = [keep.tile([P, HALF * PACK], BF16, name="wa_grouped%d" % h, align_bytes=64) for h in range(2)]
+        wa_codes = keep.tile([P, H], U32, name="wa_codes", align_bytes=64)
+        wa_scales = keep.tile([P, H], U8, name="wa_scales", align_bytes=64)
+        for h in range(2):
+            cols = slice(h * HALF, (h + 1) * HALF)
+            interleave(nc.scalar.copy, wa_grouped[h][:], wa_raw[h][:])
+            quantize(wa_codes[:, cols], wa_scales[:, cols], wa_grouped[h][:])
+        xa_words = pick_words(offs_t, "xa_words", "xa_words")
+        xb_picked = pick_scales(two_t, "xb_scales")
+        xb_scales = deal_scales(xb_picked, "xb_scales")
+
+        a_rows = {}
+        pa = [keep.tile([P, W], F32, name="pa%d" % t) for t in range(PACK)]
+        pb = [keep.tile([P, W], F32, name="pb%d" % t) for t in range(PACK)]
+        dt = {}
+        a_tags = ["first_rows", "a_rows1", "handed_on", "handed_on"]
+        z2_rows = keep.tile([P, PACK, N], BF16, name="z2_rows")
+
+        def project_a(t, pieces):
+            tokens = slice(t * P, (t + 1) * P)
+            width = H // pieces
+            a_rows[t] = keep.tile([P, H], F32, name="a_rows%d" % t, tag=a_tags[t], align_bytes=64)
+            for piece in range(pieces):
+                cols = slice(piece * width, (piece + 1) * width)
+                acc = psum.tile([P, H], F32, name="acc")
+                product(acc[:, :width], xa_words[:, tokens], xa_scales[:, tokens], wa_codes[:, cols], wa_scales[:, cols])
+                nc.scalar.copy(a_rows[t][:, cols], acc[:, :width])
+
+        def fetch_scalar(dst, window, offsets, func):
+            nc.scalar.activation(dst, window.indirect(offsets), func)
+
+        def scatter(t, offsets, op):
+            nc.vector.tensor_tensor(dt[t][:].indirect(offsets[:]), pa[t][:], pb[t][:], op)
+
+        def z_views(t):
+            return (
+                z_rows[:, t, :].rearrange("p (u m) -> p m u", u=PACK),
+                dt[t][:].rearrange("p (m u) -> p m u", u=PACK),
+            )
+
+        def weigh_z_scalar(t):
+            dst, src = z_views(t)
+            nc.scalar.activation(dst, src, ACT.Copy, scale=gt_t[:, t : t + 1])
+
+        project_a(0, 2)
+        fetch_scalar(pa[0][:], a_rows[0][:], n1_t[:], ACT.Copy)
+        nc.vector.tensor_copy(pb[0][:], a_rows[0][:].indirect(n2_t[:]))
+        dt[0] = keep.tile([P, H], F32, name="dt0")
+        scatter(0, n1_t, ALU.add)
+        xb_words = pick_words(two_t, "xb_words", "first_rows")
+        scatter(0, n2_t, ALU.mult)
+
+        def prepare(t):
+            project_a(t, 1)
+            fetch_scalar(pa[t][:], a_rows[t][:], n1_t[:], ACT.Copy)
+            fetch_scalar(pb[t][:], a_rows[t][:], n2_t[:], ACT.Copy)
+
+        prepare(1)
+        wb_grouped = keep.tile([P, N * PACK], BF16, name="wb_grouped", tag="wb_then_dt", align_bytes=64)
+        wb_codes = keep.tile([P, N], U32, name="wb_codes", align_bytes=64)
+        wb_scales = keep.tile([P, N], U8, name="wb_scales", align_bytes=64)
+        for h in range(2):
+            interleave(
+                nc.scalar.copy,
+                wb_grouped[:, h * HALF * PACK : (h + 1) * HALF * PACK],
+                wb_raw[:, :, h * HALF : (h + 1) * HALF],
+            )
+        quantize(wb_codes[:], wb_scales[:], wb_grouped[:])
+        dt[1] = keep.tile([P, H], F32, name="dt1", tag="wb_then_dt", align_bytes=64)
+        scatter(1, n1_t, ALU.add)
+        scatter(1, n2_t, ALU.mult)
+        prepare(2)
+        prepare(3)
+        dt[2] = keep.tile([P, H], F32, name="dt2", tag="handed_on", align_bytes=64)
+        dt[3] = keep.tile([P, H], F32, name="dt3")
+        scatter(2, n1_t, ALU.add)
+        scatter(3, n1_t, ALU.add)
+        scatter(2, n2_t, ALU.mult)
+        scatter(3, n2_t, ALU.mult)
+        for t in range(PACK):
+            tokens = slice(t * P, (t + 1) * P)
+            acc = psum.tile([P, N], F32, name="acc")
+            product(acc[:], xb_words[:, tokens], xb_scales[:, tokens], wb_codes[:], wb_scales[:])
+            nc.scalar.activation(z2_rows[:, t, :], acc[:], ACT.Copy, scale=gi_t[:, t : t + 1])
+        z_rows = keep.tile([P, PACK, H], BF16, name="z_rows", tag="first_rows", align_bytes=64)
+        z2_grouped = keep.tile([P, N * PACK], BF16, name="z2_grouped", align_bytes=64)
+        z2_codes = keep.tile([P, N], U32, name="z2_codes", align_bytes=64)
+        z2_scales = keep.tile([P, N], U8, name="z2_scales", align_bytes=64)
+        for h in range(2):
+            weigh_z_scalar(h)
+            interleave(
+                nc.scalar.copy,
+                z2_grouped[:, h * HALF * PACK : (h + 1) * HALF * PACK],
+                z2_rows[:, :, h * HALF : (h + 1) * HALF],
+            )
+        weigh_z_scalar(2)
+        weigh_z_scalar(3)
+
+        for h in range(2):
+            cols = slice(h * HALF, (h + 1) * HALF)
+            quantize(z2_codes[:, cols], z2_scales[:, cols], z2_grouped[:, h * HALF * PACK : (h + 1) * HALF * PACK])
+
+        z_grouped = [keep.tile([P, P * PACK], BF16, name="z_grouped%d" % u, align_bytes=64) for u in range(PACK)]
+        z_codes = [keep.tile([P, P], U32, name="z_codes%d" % u, align_bytes=64) for u in range(PACK)]
+        z_scales = [keep.tile([P, P], U8, name="z_scales%d" % u, align_bytes=64) for u in range(PACK)]
+        cv_acc = []
+        for u in range(PACK):
+            interleave(nc.vector.tensor_copy, z_grouped[u][:], z_rows[:, :, u * P : (u + 1) * P])
+            quantize(z_codes[u][:], z_scales[u][:], z_grouped[u][:])
+            acc = psum.tile([P, N], F32, name="acc")
+            product(acc[:], z_codes[u][:], z_scales[u][:], z2_codes[:], z2_scales[:])
+            cv_acc.append(acc)
+
+        out_rows = out.rearrange("(p u) n -> u p n", u=PACK)
+        cv = [keep.tile([P, N], F32, name="cv%d" % u) for u in range(PACK)]
+        gate = [keep.tile([P, N], F32, name="gate%d" % u) for u in range(PACK)]
+        other = [keep.tile([P, N], F32, name="other%d" % u) for u in range(PACK)]
+        diff = [keep.tile([P, N], F32, name="diff%d" % u) for u in range(PACK)]
+        result = [keep.tile([P, N], F32, name="result%d" % u) for u in range(PACK)]
+        halves = [(slice(h * HALF, (h + 1) * HALF), slice(h * HALF // 16, (h + 1) * HALF // 16)) for h in range(2)]
+
+        picked_gate = [keep.tile([P, N], F32, name="picked_gate%d" % u) for u in range(PACK)]
+
+        def cv_out_vector(u):
+            nc.vector.tensor_scalar(cv[u][:], cv_acc[u][:], 0.0625, None, ALU.mult)
+
+        def fetch_other(u, h):
+            cols, entries = halves[h]
+            fetch_scalar(other[u][:, cols], cv[u][:], n3_t[:, entries], ACT.Copy)
+
+        def fetch_gate(u, h):
+            cols, entries = halves[h]
+            fetch_scalar(picked_gate[u][:, cols], cv[u][:], n4_t[:, entries], ACT.Sigmoid)
+
+        def subtract(u, h):
+            cols, entries = halves[h]
+            nc.vector.tensor_tensor(diff[u][:, cols], cv[u][:, cols], other[u][:, cols], ALU.subtract)
+
+        def finish_fused(u, h):
+            cols, entries = halves[h]
+            nc.vector.tensor_tensor(result[u][:, cols], gate[u][:].indirect(n4_t[:, entries]), diff[u][:, cols], ALU.mult)
+            nc.sync.dma_start(out=out_rows[u][:, cols], in_=result[u][:, cols])
+
+        def finish_plain(u, h):
+            cols, entries = halves[h]
+            nc.vector.tensor_tensor(result[u][:, cols], picked_gate[u][:, cols], diff[u][:, cols], ALU.mult)
+            nc.sync.dma_start(out=out_rows[u][:, cols], in_=result[u][:, cols])
+
+        nc.scalar.activation(gate[0][:], cv_acc[0][:], ACT.Sigmoid, scale=0.0625)
+        nc.scalar.activation(cv[0][:], cv_acc[0][:], ACT.Copy, scale=0.0625)
+        for u in range(1, PACK):
+            cv_out_vector(u)
+        for h in range(2):
+            fetch_other(0, h)
+        nc.scalar.activation(gate[1][:], cv[1][:], ACT.Sigmoid)
+        for h in range(2):
+            fetch_other(1, h)
+        for u in range(2):
+            for h in range(2):
+                subtract(u, h)
+            for h in range(2):
+                finish_fused(u, h)
+        for u in range(2, PACK):
+            for h in range(2):
+                fetch_other(u, h)
+                fetch_gate(u, h)
+                subtract(u, h)
+                finish_plain(u, h)

@@ -17,8 +17,14 @@ ALU = mybir.AluOpType
 
 P = 128
 PACK = 4
+QUADRANT = 32
+SCALE_ROWS = 4
+GROUP = 16
 HALF = 256
-VECTOR_COLUMNS = 160
+LINE = 4
+PSUM_BANKS = 8
+CV_FACTOR = 0.0625
+VECTOR_GATED = 2
 
 
 def tile_picked_mombondgdif_none_p_kernel(
@@ -27,7 +33,7 @@ def tile_picked_mombondgdif_none_p_kernel(
     nc = tc.nc
     with ExitStack() as ctx:
         keep = ctx.enter_context(tc.tile_pool(name="keep", bufs=1))
-        psum = ctx.enter_context(tc.psum_pool(name="psum", bufs=8))
+        psum = ctx.enter_context(tc.psum_pool(name="psum", bufs=PSUM_BANKS))
 
         def load_list(src, name):
             tile = keep.tile(list(src.shape), U16, name=name)
@@ -40,15 +46,15 @@ def tile_picked_mombondgdif_none_p_kernel(
             nc.sync.dma_start(out=tile[:], in_=rows[:, :, half * HALF : (half + 1) * HALF])
             return tile
 
-        def load_gate(g, name):
+        def load_place_weights(g, name):
             tile = keep.tile([P, PACK], F32, name=name)
             nc.sync.dma_start(out=tile[:], in_=g.rearrange("(p t) o -> p (t o)", t=PACK))
             return tile
 
-        def interleave(copy, dst, src):
+        def interleave(copy, grouped, rows):
             copy(
-                out=dst.rearrange("p (c i t) -> p c t i", i=4, t=PACK),
-                in_=src.rearrange("p t (c i) -> p c t i", i=4),
+                out=grouped.rearrange("p (c i t) -> p c t i", i=LINE, t=PACK),
+                in_=rows.rearrange("p t (c i) -> p c t i", i=LINE),
             )
 
         def quantize(codes, scales, grouped):
@@ -65,13 +71,22 @@ def tile_picked_mombondgdif_none_p_kernel(
                 stop=True,
             )
 
+        def half_columns(half):
+            return slice(half * HALF, (half + 1) * HALF)
+
+        def half_grouped(half):
+            return slice(half * HALF * PACK, (half + 1) * HALF * PACK)
+
+        def half_entries(half):
+            return slice(half * HALF // GROUP, (half + 1) * HALF // GROUP)
+
         scale_table = keep.tile([P, T], U8, name="scale_table")
         nc.vector.memset(scale_table[:].bitcast(I32), 0)
         offs_t = load_list(offs, "offs_t")
-        for q in range(4):
+        for q in range(P // QUADRANT):
             nc.sync.dma_start(
-                out=scale_table[32 * q : 32 * q + 4, :].bitcast(I32),
-                in_=x_scales[0, 4 * q : 4 * q + 4, :].bitcast(I32),
+                out=scale_table[QUADRANT * q : QUADRANT * q + SCALE_ROWS, :].bitcast(I32),
+                in_=x_scales[0, SCALE_ROWS * q : SCALE_ROWS * (q + 1), :].bitcast(I32),
             )
         wa_raw = [load_weight_half(wa, h, "wa_raw%d" % h) for h in range(2)]
         word_table = keep.tile([P, T], U32, name="word_table")
@@ -84,17 +99,14 @@ def tile_picked_mombondgdif_none_p_kernel(
         n2_t = load_list(n2, "n2_t")
         wb_raw = keep.tile([P, PACK, N], F32, name="wb_raw", tag="handed_on", align_bytes=64)
         nc.sync.dma_start(out=wb_raw[:], in_=wb.rearrange("(p j) c -> p j c", j=PACK))
-        gt_t = load_gate(gt, "gt_t")
-        gi_t = load_gate(gi, "gi_t")
+        gt_t = load_place_weights(gt, "gt_t")
+        gi_t = load_place_weights(gi, "gi_t")
         n4_t = load_list(n4, "n4_t")
         n3_t = load_list(n3, "n3_t")
 
         def pick_scales(offsets, name):
             picked = keep.tile([P, S], U8, name=name + "_picked")
             nc.vector.tensor_copy(picked[:], scale_table[:].indirect(offsets[:]))
-            return picked
-
-        def deal_scales(picked, name):
             dealt = keep.tile([P, S], U8, name=name + "_dealt", align_bytes=64)
             nc.vector.tensor_copy(
                 out=dealt[:].rearrange("p (t m) -> p t m", t=PACK),
@@ -109,19 +121,17 @@ def tile_picked_mombondgdif_none_p_kernel(
             )
             return dealt
 
-        xa_picked = pick_scales(offs_t, "xa_scales")
-        xa_scales = deal_scales(xa_picked, "xa_scales")
+        xa_scales = pick_scales(offs_t, "xa_scales")
 
         wa_grouped = [keep.tile([P, HALF * PACK], BF16, name="wa_grouped%d" % h, align_bytes=64) for h in range(2)]
         wa_codes = keep.tile([P, H], U32, name="wa_codes", align_bytes=64)
         wa_scales = keep.tile([P, H], U8, name="wa_scales", align_bytes=64)
         for h in range(2):
-            cols = slice(h * HALF, (h + 1) * HALF)
+            cols = half_columns(h)
             interleave(nc.scalar.copy, wa_grouped[h][:], wa_raw[h][:])
             quantize(wa_codes[:, cols], wa_scales[:, cols], wa_grouped[h][:])
         xa_words = pick_words(offs_t, "xa_words", "xa_words")
-        xb_picked = pick_scales(two_t, "xb_scales")
-        xb_scales = deal_scales(xb_picked, "xb_scales")
+        xb_scales = pick_scales(two_t, "xb_scales")
 
         a_rows = {}
         pa = [keep.tile([P, W], F32, name="pa%d" % t) for t in range(PACK)]
@@ -140,79 +150,71 @@ def tile_picked_mombondgdif_none_p_kernel(
                 product(acc[:, :width], xa_words[:, tokens], xa_scales[:, tokens], wa_codes[:, cols], wa_scales[:, cols])
                 nc.scalar.copy(a_rows[t][:, cols], acc[:, :width])
 
-        def fetch_scalar(dst, window, offsets, func):
+        def look_up_on_scalar(dst, window, offsets, func):
             nc.scalar.activation(dst, window.indirect(offsets), func)
 
         def scatter(t, offsets, op):
             nc.vector.tensor_tensor(dt[t][:].indirect(offsets[:]), pa[t][:], pb[t][:], op)
 
-        def z_views(t):
-            return (
-                z_rows[:, t, :].rearrange("p (u m) -> p m u", u=PACK),
-                dt[t][:].rearrange("p (m u) -> p m u", u=PACK),
-            )
-
-        def weigh_z_scalar(t):
-            dst, src = z_views(t)
-            nc.scalar.activation(dst, src, ACT.Copy, scale=gt_t[:, t : t + 1])
+        def prepare(t):
+            project_a(t, 1)
+            look_up_on_scalar(pa[t][:], a_rows[t][:], n1_t[:], ACT.Copy)
+            look_up_on_scalar(pb[t][:], a_rows[t][:], n2_t[:], ACT.Copy)
 
         project_a(0, 2)
-        fetch_scalar(pa[0][:], a_rows[0][:], n1_t[:], ACT.Copy)
+        look_up_on_scalar(pa[0][:], a_rows[0][:], n1_t[:], ACT.Copy)
         nc.vector.tensor_copy(pb[0][:], a_rows[0][:].indirect(n2_t[:]))
         dt[0] = keep.tile([P, H], F32, name="dt0")
         scatter(0, n1_t, ALU.add)
         xb_words = pick_words(two_t, "xb_words", "first_rows")
         scatter(0, n2_t, ALU.mult)
 
-        def prepare(t):
-            project_a(t, 1)
-            fetch_scalar(pa[t][:], a_rows[t][:], n1_t[:], ACT.Copy)
-            fetch_scalar(pb[t][:], a_rows[t][:], n2_t[:], ACT.Copy)
-
         prepare(1)
         wb_grouped = keep.tile([P, N * PACK], BF16, name="wb_grouped", tag="wb_then_dt", align_bytes=64)
         wb_codes = keep.tile([P, N], U32, name="wb_codes", align_bytes=64)
         wb_scales = keep.tile([P, N], U8, name="wb_scales", align_bytes=64)
         for h in range(2):
-            interleave(
-                nc.scalar.copy,
-                wb_grouped[:, h * HALF * PACK : (h + 1) * HALF * PACK],
-                wb_raw[:, :, h * HALF : (h + 1) * HALF],
-            )
+            interleave(nc.scalar.copy, wb_grouped[:, half_grouped(h)], wb_raw[:, :, half_columns(h)])
         quantize(wb_codes[:], wb_scales[:], wb_grouped[:])
         dt[1] = keep.tile([P, H], F32, name="dt1", tag="wb_then_dt", align_bytes=64)
         scatter(1, n1_t, ALU.add)
         scatter(1, n2_t, ALU.mult)
+
         prepare(2)
         prepare(3)
         dt[2] = keep.tile([P, H], F32, name="dt2", tag="handed_on", align_bytes=64)
         dt[3] = keep.tile([P, H], F32, name="dt3")
-        scatter(2, n1_t, ALU.add)
-        scatter(3, n1_t, ALU.add)
-        scatter(2, n2_t, ALU.mult)
-        scatter(3, n2_t, ALU.mult)
+        for offsets, op in ((n1_t, ALU.add), (n2_t, ALU.mult)):
+            for t in (2, 3):
+                scatter(t, offsets, op)
+
         for t in range(PACK):
             tokens = slice(t * P, (t + 1) * P)
             acc = psum.tile([P, N], F32, name="acc")
             product(acc[:], xb_words[:, tokens], xb_scales[:, tokens], wb_codes[:], wb_scales[:])
             nc.scalar.activation(z2_rows[:, t, :], acc[:], ACT.Copy, scale=gi_t[:, t : t + 1])
+
         z_rows = keep.tile([P, PACK, H], BF16, name="z_rows", tag="first_rows", align_bytes=64)
         z2_grouped = keep.tile([P, N * PACK], BF16, name="z2_grouped", align_bytes=64)
         z2_codes = keep.tile([P, N], U32, name="z2_codes", align_bytes=64)
         z2_scales = keep.tile([P, N], U8, name="z2_scales", align_bytes=64)
-        for h in range(2):
-            weigh_z_scalar(h)
-            interleave(
-                nc.scalar.copy,
-                z2_grouped[:, h * HALF * PACK : (h + 1) * HALF * PACK],
-                z2_rows[:, :, h * HALF : (h + 1) * HALF],
+
+        def weigh_z(t):
+            nc.scalar.activation(
+                z_rows[:, t, :].rearrange("p (u m) -> p m u", u=PACK),
+                dt[t][:].rearrange("p (m u) -> p m u", u=PACK),
+                ACT.Copy,
+                scale=gt_t[:, t : t + 1],
             )
-        weigh_z_scalar(2)
-        weigh_z_scalar(3)
 
         for h in range(2):
-            cols = slice(h * HALF, (h + 1) * HALF)
-            quantize(z2_codes[:, cols], z2_scales[:, cols], z2_grouped[:, h * HALF * PACK : (h + 1) * HALF * PACK])
+            weigh_z(h)
+            interleave(nc.scalar.copy, z2_grouped[:, half_grouped(h)], z2_rows[:, :, half_columns(h)])
+        weigh_z(2)
+        weigh_z(3)
+        for h in range(2):
+            cols = half_columns(h)
+            quantize(z2_codes[:, cols], z2_scales[:, cols], z2_grouped[:, half_grouped(h)])
 
         z_grouped = [keep.tile([P, P * PACK], BF16, name="z_grouped%d" % u, align_bytes=64) for u in range(PACK)]
         z_codes = [keep.tile([P, P], U32, name="z_codes%d" % u, align_bytes=64) for u in range(PACK)]
@@ -227,56 +229,42 @@ def tile_picked_mombondgdif_none_p_kernel(
 
         out_rows = out.rearrange("(p u) n -> u p n", u=PACK)
         cv = [keep.tile([P, N], F32, name="cv%d" % u) for u in range(PACK)]
-        gate = [keep.tile([P, N], F32, name="gate%d" % u) for u in range(PACK)]
-        other = [keep.tile([P, N], F32, name="other%d" % u) for u in range(PACK)]
+        sigmoid_rows = [keep.tile([P, N], F32, name="gate%d" % u) for u in range(VECTOR_GATED)]
+        cv_at_n3 = [keep.tile([P, N], F32, name="other%d" % u) for u in range(PACK)]
         diff = [keep.tile([P, N], F32, name="diff%d" % u) for u in range(PACK)]
         result = [keep.tile([P, N], F32, name="result%d" % u) for u in range(PACK)]
-        halves = [(slice(h * HALF, (h + 1) * HALF), slice(h * HALF // 16, (h + 1) * HALF // 16)) for h in range(2)]
+        sigmoid_at_n4 = {u: keep.tile([P, N], F32, name="picked_gate%d" % u) for u in range(VECTOR_GATED, PACK)}
 
-        picked_gate = [keep.tile([P, N], F32, name="picked_gate%d" % u) for u in range(PACK)]
-
-        def cv_out_vector(u):
-            nc.vector.tensor_scalar(cv[u][:], cv_acc[u][:], 0.0625, None, ALU.mult)
-
-        def fetch_other(u, h):
-            cols, entries = halves[h]
-            fetch_scalar(other[u][:, cols], cv[u][:], n3_t[:, entries], ACT.Copy)
-
-        def fetch_gate(u, h):
-            cols, entries = halves[h]
-            fetch_scalar(picked_gate[u][:, cols], cv[u][:], n4_t[:, entries], ACT.Sigmoid)
+        def look_up_n3(u, h):
+            look_up_on_scalar(cv_at_n3[u][:, half_columns(h)], cv[u][:], n3_t[:, half_entries(h)], ACT.Copy)
 
         def subtract(u, h):
-            cols, entries = halves[h]
-            nc.vector.tensor_tensor(diff[u][:, cols], cv[u][:, cols], other[u][:, cols], ALU.subtract)
+            cols = half_columns(h)
+            nc.vector.tensor_tensor(diff[u][:, cols], cv[u][:, cols], cv_at_n3[u][:, cols], ALU.subtract)
 
-        def finish_fused(u, h):
-            cols, entries = halves[h]
-            nc.vector.tensor_tensor(result[u][:, cols], gate[u][:].indirect(n4_t[:, entries]), diff[u][:, cols], ALU.mult)
+        def finish(u, h, factor):
+            cols = half_columns(h)
+            nc.vector.tensor_tensor(result[u][:, cols], factor, diff[u][:, cols], ALU.mult)
             nc.sync.dma_start(out=out_rows[u][:, cols], in_=result[u][:, cols])
 
-        def finish_plain(u, h):
-            cols, entries = halves[h]
-            nc.vector.tensor_tensor(result[u][:, cols], picked_gate[u][:, cols], diff[u][:, cols], ALU.mult)
-            nc.sync.dma_start(out=out_rows[u][:, cols], in_=result[u][:, cols])
-
-        nc.scalar.activation(gate[0][:], cv_acc[0][:], ACT.Sigmoid, scale=0.0625)
-        nc.scalar.activation(cv[0][:], cv_acc[0][:], ACT.Copy, scale=0.0625)
+        nc.scalar.activation(sigmoid_rows[0][:], cv_acc[0][:], ACT.Sigmoid, scale=CV_FACTOR)
+        nc.scalar.activation(cv[0][:], cv_acc[0][:], ACT.Copy, scale=CV_FACTOR)
         for u in range(1, PACK):
-            cv_out_vector(u)
-        for h in range(2):
-            fetch_other(0, h)
-        nc.scalar.activation(gate[1][:], cv[1][:], ACT.Sigmoid)
-        for h in range(2):
-            fetch_other(1, h)
-        for u in range(2):
+            nc.vector.tensor_scalar(cv[u][:], cv_acc[u][:], CV_FACTOR, None, ALU.mult)
+        for u in range(VECTOR_GATED):
+            if u > 0:
+                nc.scalar.activation(sigmoid_rows[u][:], cv[u][:], ACT.Sigmoid)
+            for h in range(2):
+                look_up_n3(u, h)
+        for u in range(VECTOR_GATED):
             for h in range(2):
                 subtract(u, h)
             for h in range(2):
-                finish_fused(u, h)
-        for u in range(2, PACK):
+                finish(u, h, sigmoid_rows[u][:].indirect(n4_t[:, half_entries(h)]))
+        for u in range(VECTOR_GATED, PACK):
             for h in range(2):
-                fetch_other(u, h)
-                fetch_gate(u, h)
+                factor = sigmoid_at_n4[u][:, half_columns(h)]
+                look_up_n3(u, h)
+                look_up_on_scalar(factor, cv[u][:], n4_t[:, half_entries(h)], ACT.Sigmoid)
                 subtract(u, h)
-                finish_plain(u, h)
+                finish(u, h, factor)

from contextlib import ExitStack

import concourse.mybir as mybir

K, T, S, N, H, W = 512, 2048, 512, 512, 512, 256
FLOPS = 2 * K * S * H + 2 * K * S * N + 2 * S * H * N

F32 = mybir.dt.float32
BF16 = mybir.dt.bfloat16
I32 = mybir.dt.int32
U32 = mybir.dt.uint32
U16 = mybir.dt.uint16
U8 = mybir.dt.uint8
FP8X4 = mybir.dt.float8_e4m3fn_x4
ACT = mybir.ActivationFunctionType
ALU = mybir.AluOpType

P = 128
PACK = 4
QUADRANT = 32
SCALE_ROWS = 4
GROUP = 16
HALF = 256
LINE = 4
PSUM_BANKS = 8
CV_FACTOR = 0.0625
VECTOR_GATED = 2


def tile_picked_mombondgdif_none_p_kernel(
    tc, x_words, x_scales, wa, wb, gt, gi, offs, two, n1, n2, n3, n4, out
):
    nc = tc.nc
    with ExitStack() as ctx:
        keep = ctx.enter_context(tc.tile_pool(name="keep", bufs=1))
        psum = ctx.enter_context(tc.psum_pool(name="psum", bufs=PSUM_BANKS))

        def load_list(src, name):
            tile = keep.tile(list(src.shape), U16, name=name)
            nc.sync.dma_start(tile[:], src)
            return tile

        def load_weight_half(w, half, name):
            tile = keep.tile([P, PACK, HALF], F32, name=name)
            rows = w.rearrange("(p j) c -> p j c", j=PACK)
            nc.sync.dma_start(out=tile[:], in_=rows[:, :, half * HALF : (half + 1) * HALF])
            return tile

        def load_place_weights(g, name):
            tile = keep.tile([P, PACK], F32, name=name)
            nc.sync.dma_start(out=tile[:], in_=g.rearrange("(p t) o -> p (t o)", t=PACK))
            return tile

        def interleave(copy, grouped, rows):
            copy(
                out=grouped.rearrange("p (c i t) -> p c t i", i=LINE, t=PACK),
                in_=rows.rearrange("p t (c i) -> p c t i", i=LINE),
            )

        def quantize(codes, scales, grouped):
            nc.vector.quantize_mx(out=codes.bitcast(FP8X4), scales=scales, in_=grouped)

        def product(acc, left_codes, left_scales, right_codes, right_scales):
            nc.tensor.matmul_mx(
                out=acc,
                lhsT=left_codes.bitcast(FP8X4),
                lhsT_scale=left_scales,
                rhs=right_codes.bitcast(FP8X4),
                rhs_scale=right_scales,
                start=True,
                stop=True,
            )

        def half_columns(half):
            return slice(half * HALF, (half + 1) * HALF)

        def half_grouped(half):
            return slice(half * HALF * PACK, (half + 1) * HALF * PACK)

        def half_entries(half):
            return slice(half * HALF // GROUP, (half + 1) * HALF // GROUP)

        scale_table = keep.tile([P, T], U8, name="scale_table")
        nc.vector.memset(scale_table[:].bitcast(I32), 0)
        offs_t = load_list(offs, "offs_t")
        for q in range(P // QUADRANT):
            nc.sync.dma_start(
                out=scale_table[QUADRANT * q : QUADRANT * q + SCALE_ROWS, :].bitcast(I32),
                in_=x_scales[0, SCALE_ROWS * q : SCALE_ROWS * (q + 1), :].bitcast(I32),
            )
        wa_raw = [load_weight_half(wa, h, "wa_raw%d" % h) for h in range(2)]
        word_table = keep.tile([P, T], U32, name="word_table")
        nc.sync.dma_start(
            out=word_table[:].bitcast(I32),
            in_=x_words[0].rearrange("p n t -> p (n t)").bitcast(I32),
        )
        two_t = load_list(two, "two_t")
        n1_t = load_list(n1, "n1_t")
        n2_t = load_list(n2, "n2_t")
        wb_raw = keep.tile([P, PACK, N], F32, name="wb_raw", tag="handed_on", align_bytes=64)
        nc.sync.dma_start(out=wb_raw[:], in_=wb.rearrange("(p j) c -> p j c", j=PACK))
        gt_t = load_place_weights(gt, "gt_t")
        gi_t = load_place_weights(gi, "gi_t")
        n4_t = load_list(n4, "n4_t")
        n3_t = load_list(n3, "n3_t")

        def pick_scales(offsets, name):
            picked = keep.tile([P, S], U8, name=name + "_picked")
            nc.vector.tensor_copy(picked[:], scale_table[:].indirect(offsets[:]))
            dealt = keep.tile([P, S], U8, name=name + "_dealt", align_bytes=64)
            nc.vector.tensor_copy(
                out=dealt[:].rearrange("p (t m) -> p t m", t=PACK),
                in_=picked[:].rearrange("p (m t) -> p t m", t=PACK),
            )
            return dealt

        def pick_words(offsets, name, tag):
            dealt = keep.tile([P, S], U32, name=name, tag=tag, align_bytes=64)
            nc.vector.tensor_copy(
                dealt[:].rearrange("p (t m) -> p m t", t=PACK), word_table[:].indirect(offsets[:])
            )
            return dealt

        xa_scales = pick_scales(offs_t, "xa_scales")

        wa_grouped = [keep.tile([P, HALF * PACK], BF16, name="wa_grouped%d" % h, align_bytes=64) for h in range(2)]
        wa_codes = keep.tile([P, H], U32, name="wa_codes", align_bytes=64)
        wa_scales = keep.tile([P, H], U8, name="wa_scales", align_bytes=64)
        for h in range(2):
            cols = half_columns(h)
            interleave(nc.scalar.copy, wa_grouped[h][:], wa_raw[h][:])
            quantize(wa_codes[:, cols], wa_scales[:, cols], wa_grouped[h][:])
        xa_words = pick_words(offs_t, "xa_words", "xa_words")
        xb_scales = pick_scales(two_t, "xb_scales")

        a_rows = {}
        pa = [keep.tile([P, W], F32, name="pa%d" % t) for t in range(PACK)]
        pb = [keep.tile([P, W], F32, name="pb%d" % t) for t in range(PACK)]
        dt = {}
        a_tags = ["first_rows", "a_rows1", "handed_on", "handed_on"]
        z2_rows = keep.tile([P, PACK, N], BF16, name="z2_rows")

        def project_a(t, pieces):
            tokens = slice(t * P, (t + 1) * P)
            width = H // pieces
            a_rows[t] = keep.tile([P, H], F32, name="a_rows%d" % t, tag=a_tags[t], align_bytes=64)
            for piece in range(pieces):
                cols = slice(piece * width, (piece + 1) * width)
                acc = psum.tile([P, H], F32, name="acc")
                product(acc[:, :width], xa_words[:, tokens], xa_scales[:, tokens], wa_codes[:, cols], wa_scales[:, cols])
                nc.scalar.copy(a_rows[t][:, cols], acc[:, :width])

        def look_up_on_scalar(dst, window, offsets, func):
            nc.scalar.activation(dst, window.indirect(offsets), func)

        def scatter(t, offsets, op):
            nc.vector.tensor_tensor(dt[t][:].indirect(offsets[:]), pa[t][:], pb[t][:], op)

        def prepare(t):
            project_a(t, 1)
            look_up_on_scalar(pa[t][:], a_rows[t][:], n1_t[:], ACT.Copy)
            look_up_on_scalar(pb[t][:], a_rows[t][:], n2_t[:], ACT.Copy)

        project_a(0, 2)
        look_up_on_scalar(pa[0][:], a_rows[0][:], n1_t[:], ACT.Copy)
        nc.vector.tensor_copy(pb[0][:], a_rows[0][:].indirect(n2_t[:]))
        dt[0] = keep.tile([P, H], F32, name="dt0")
        scatter(0, n1_t, ALU.add)
        xb_words = pick_words(two_t, "xb_words", "first_rows")
        scatter(0, n2_t, ALU.mult)

        prepare(1)
        wb_grouped = keep.tile([P, N * PACK], BF16, name="wb_grouped", tag="wb_then_dt", align_bytes=64)
        wb_codes = keep.tile([P, N], U32, name="wb_codes", align_bytes=64)
        wb_scales = keep.tile([P, N], U8, name="wb_scales", align_bytes=64)
        for h in range(2):
            interleave(nc.scalar.copy, wb_grouped[:, half_grouped(h)], wb_raw[:, :, half_columns(h)])
        quantize(wb_codes[:], wb_scales[:], wb_grouped[:])
        dt[1] = keep.tile([P, H], F32, name="dt1", tag="wb_then_dt", align_bytes=64)
        scatter(1, n1_t, ALU.add)
        scatter(1, n2_t, ALU.mult)

        prepare(2)
        prepare(3)
        dt[2] = keep.tile([P, H], F32, name="dt2", tag="handed_on", align_bytes=64)
        dt[3] = keep.tile([P, H], F32, name="dt3")
        for offsets, op in ((n1_t, ALU.add), (n2_t, ALU.mult)):
            for t in (2, 3):
                scatter(t, offsets, op)

        for t in range(PACK):
            tokens = slice(t * P, (t + 1) * P)
            acc = psum.tile([P, N], F32, name="acc")
            product(acc[:], xb_words[:, tokens], xb_scales[:, tokens], wb_codes[:], wb_scales[:])
            nc.scalar.activation(z2_rows[:, t, :], acc[:], ACT.Copy, scale=gi_t[:, t : t + 1])

        z_rows = keep.tile([P, PACK, H], BF16, name="z_rows", tag="first_rows", align_bytes=64)
        z2_grouped = keep.tile([P, N * PACK], BF16, name="z2_grouped", align_bytes=64)
        z2_codes = keep.tile([P, N], U32, name="z2_codes", align_bytes=64)
        z2_scales = keep.tile([P, N], U8, name="z2_scales", align_bytes=64)

        def weigh_z(t):
            nc.scalar.activation(
                z_rows[:, t, :].rearrange("p (u m) -> p m u", u=PACK),
                dt[t][:].rearrange("p (m u) -> p m u", u=PACK),
                ACT.Copy,
                scale=gt_t[:, t : t + 1],
            )

        for h in range(2):
            weigh_z(h)
            interleave(nc.scalar.copy, z2_grouped[:, half_grouped(h)], z2_rows[:, :, half_columns(h)])
        weigh_z(2)
        weigh_z(3)
        for h in range(2):
            cols = half_columns(h)
            quantize(z2_codes[:, cols], z2_scales[:, cols], z2_grouped[:, half_grouped(h)])

        z_grouped = [keep.tile([P, P * PACK], BF16, name="z_grouped%d" % u, align_bytes=64) for u in range(PACK)]
        z_codes = [keep.tile([P, P], U32, name="z_codes%d" % u, align_bytes=64) for u in range(PACK)]
        z_scales = [keep.tile([P, P], U8, name="z_scales%d" % u, align_bytes=64) for u in range(PACK)]
        cv_acc = []
        for u in range(PACK):
            interleave(nc.vector.tensor_copy, z_grouped[u][:], z_rows[:, :, u * P : (u + 1) * P])
            quantize(z_codes[u][:], z_scales[u][:], z_grouped[u][:])
            acc = psum.tile([P, N], F32, name="acc")
            product(acc[:], z_codes[u][:], z_scales[u][:], z2_codes[:], z2_scales[:])
            cv_acc.append(acc)

        out_rows = out.rearrange("(p u) n -> u p n", u=PACK)
        cv = [keep.tile([P, N], F32, name="cv%d" % u) for u in range(PACK)]
        sigmoid_rows = [keep.tile([P, N], F32, name="gate%d" % u) for u in range(VECTOR_GATED)]
        cv_at_n3 = [keep.tile([P, N], F32, name="other%d" % u) for u in range(PACK)]
        diff = [keep.tile([P, N], F32, name="diff%d" % u) for u in range(PACK)]
        result = [keep.tile([P, N], F32, name="result%d" % u) for u in range(PACK)]
        sigmoid_at_n4 = {u: keep.tile([P, N], F32, name="picked_gate%d" % u) for u in range(VECTOR_GATED, PACK)}

        def look_up_n3(u, h):
            look_up_on_scalar(cv_at_n3[u][:, half_columns(h)], cv[u][:], n3_t[:, half_entries(h)], ACT.Copy)

        def subtract(u, h):
            cols = half_columns(h)
            nc.vector.tensor_tensor(diff[u][:, cols], cv[u][:, cols], cv_at_n3[u][:, cols], ALU.subtract)

        def finish(u, h, factor):
            cols = half_columns(h)
            nc.vector.tensor_tensor(result[u][:, cols], factor, diff[u][:, cols], ALU.mult)
            nc.sync.dma_start(out=out_rows[u][:, cols], in_=result[u][:, cols])

        nc.scalar.activation(sigmoid_rows[0][:], cv_acc[0][:], ACT.Sigmoid, scale=CV_FACTOR)
        nc.scalar.activation(cv[0][:], cv_acc[0][:], ACT.Copy, scale=CV_FACTOR)
        for u in range(1, PACK):
            nc.vector.tensor_scalar(cv[u][:], cv_acc[u][:], CV_FACTOR, None, ALU.mult)
        for u in range(VECTOR_GATED):
            if u > 0:
                nc.scalar.activation(sigmoid_rows[u][:], cv[u][:], ACT.Sigmoid)
            for h in range(2):
                look_up_n3(u, h)
        for u in range(VECTOR_GATED):
            for h in range(2):
                subtract(u, h)
            for h in range(2):
                finish(u, h, sigmoid_rows[u][:].indirect(n4_t[:, half_entries(h)]))
        for u in range(VECTOR_GATED, PACK):
            for h in range(2):
                factor = sigmoid_at_n4[u][:, half_columns(h)]
                look_up_n3(u, h)
                look_up_on_scalar(factor, cv[u][:], n4_t[:, half_entries(h)], ACT.Sigmoid)
                subtract(u, h)
                finish(u, h, factor)
